import numpy as np
import ml_dtypes


def mxq(x, axis, fmt="e4m3"):
    dtype, down = {"e4m3": (ml_dtypes.float8_e4m3fn, 7), "e5m2": (ml_dtypes.float8_e5m2, 14)}[fmt]
    v = np.moveaxis(np.asarray(x, np.float32).astype(ml_dtypes.bfloat16).astype(np.float64), axis, -1)
    blocks = v.reshape(v.shape[:-1] + (-1, 32))
    amax = np.abs(blocks).max(-1, keepdims=True)
    byte = np.maximum(np.where(amax > 0, np.frexp(amax)[1] - 1 + 127, 0) - down, 1)
    scale = np.exp2(byte - 127.0)
    codes = (blocks / scale).astype(np.float32).astype(dtype).astype(np.float64)
    return np.moveaxis((codes * scale).reshape(v.shape), -1, axis)


WIDE = False


def mx_kscale(k):
    if not WIDE:
        return np.ones(k)
    levels = np.array([10, -10, 5, -5, 0])
    if k % 512:
        return np.exp2(np.random.permutation(np.resize(levels, k // 32))).repeat(32)
    a = np.empty((k // 512, 16))
    for p in range(k // 512):
        a[p, :8] = np.random.permutation(np.resize(levels, 8))
        for g in range(8):
            far = levels[np.abs(levels - a[p, g]) >= 10]
            a[p, g + 8] = far[np.random.randint(len(far))]
    return np.exp2(a.ravel()).repeat(32)


def f64(x):
    return np.asarray(x).astype(np.float64)


def striped(idx):
    return np.tile(idx.reshape(-1, 16).T, (8, 1)).astype(np.uint16)


def unstriped(offs):
    return offs[:16].T.reshape(-1).astype(np.int64)


def striped8(idx):
    return np.concatenate([x.reshape(-1, 16).T for x in idx]).astype(np.uint16)


def runs(offs, k):
    lists = np.stack([offs[16 * r : 16 * r + 16].T.reshape(-1) for r in range(8)]).astype(np.int64)
    return lists[np.arange(k) % 512 // 64]


def pack_weight(w):
    k, n = w.shape
    w = f64(np.asarray(w, np.float32).astype(ml_dtypes.bfloat16)).reshape(k // 32, 32, n)
    amax = np.abs(w).max(1)
    byte = np.clip(np.where(amax > 0, np.frexp(amax)[1] - 1 + 127 - 7, 1), 1, 254)
    scaled = (w * np.exp2(127.0 - byte)[:, None, :]).reshape(k, n).astype(np.float32)
    words = np.ascontiguousarray(scaled.reshape(k // 512, 128, 4, n).transpose(0, 1, 3, 2)).astype(ml_dtypes.float8_e4m3fn).view(np.uint8)
    return words, np.ascontiguousarray(byte.astype(np.uint8).reshape(k // 512, 16, n))


def unpack_weight(words, scales):
    g, p, n, _ = words.shape
    vals = np.ascontiguousarray(words).view(ml_dtypes.float8_e4m3fn).astype(np.float64) * np.repeat(np.exp2(scales.astype(np.float64) - 127.0), 8, axis=1)[..., None]
    return vals.transpose(0, 1, 3, 2).reshape(g * 512, n)


K, T, S, G, H, W = 512, 1024, 512, 2048, 512, 256


def setup_inputs():
    n = np.random.standard_normal
    s = mx_kscale(K)[:, None]
    packed_xT = pack_weight(n((K, T)) * s)
    packed_dT = pack_weight(n((K, G)) / s)
    perm = np.stack([np.random.permutation(S) for _ in range(8)])
    perm2 = np.stack([np.random.permutation(S) for _ in range(8)])
    perm3 = np.stack([np.random.permutation(S) for _ in range(8)])
    return {
        "x_words": packed_xT[0],
        "x_scales": packed_xT[1],
        "d_words": packed_dT[0],
        "d_scales": packed_dT[1],
        "gs": (np.random.uniform(0.5, 1.5, (K, 1)) * s).astype(np.float32),
        "offs": striped(np.random.permutation(T)[:S]),
        "k1": striped8(np.random.randint(0, G, (8, H))),
        "hz": striped8(np.random.randint(0, T, (8, S))),
        "k2": striped8(np.random.randint(0, G, (8, H))),
        "n1": striped8(perm[:, :W]),
        "n2": striped8(perm[:, W:]),
        "n3": striped8(perm2[:, :W]),
        "n4": striped8(perm2[:, W:]),
        "n5": striped8(np.stack([np.random.permutation(S) for _ in range(8)])),
        "k3": striped8(np.random.randint(0, G, (8, H))),
        "k4": striped8(np.random.randint(0, G, (8, H))),
        "two": striped(np.random.permutation(T)[:S]),
        "k5": striped8(np.random.randint(0, G, (8, H))),
        "hy": striped8(np.random.randint(0, T, (8, S))),
        "n6": striped8(perm3[:, :W]),
        "n7": striped8(perm3[:, W:]),
        "n8": striped8(np.stack([np.random.permutation(S) for _ in range(8)])),
    }


def reference(x_words, x_scales, d_words, d_scales, gs, offs, k1, hz, k2, n1, n2, n3, n4, n5, k3, k4, two, k5, hy, n6, n7, n8):
    d_k3 = unpack_weight(d_words, d_scales)[np.arange(K)[:, None], runs(k3, K)]
    d_k1 = unpack_weight(d_words, d_scales)[np.arange(K)[:, None], runs(k1, K)]
    xq = unpack_weight(x_words, x_scales)[:, unstriped(offs)]
    d_k2 = unpack_weight(d_words, d_scales)[np.arange(K)[:, None], runs(k2, K)]
    x_hz = unpack_weight(x_words, x_scales)[np.arange(K)[:, None], runs(hz, K)]
    h = 0.0625 * (d_k1.T @ xq + d_k2.T @ x_hz)
    pa = h[np.arange(H)[:, None], runs(n1, H)]
    pb = h[np.arange(H)[:, None], runs(n2, H)]
    rb = np.minimum(pa, pb)
    ra = pa - pb
    ua = np.zeros((H, S))
    ua[np.arange(H)[:, None], runs(n3, H)] = ra
    ub = ua.copy()
    ub[np.arange(H)[:, None], runs(n4, H)] = rb
    z = f64(gs) * (np.maximum(ub, ub[np.arange(H)[:, None], runs(n5, H)]))
    d_k4 = unpack_weight(d_words, d_scales)[np.arange(K)[:, None], runs(k4, K)]
    x_two = unpack_weight(x_words, x_scales)[:, unstriped(two)]
    d_k5 = unpack_weight(d_words, d_scales)[np.arange(K)[:, None], runs(k5, K)]
    x_hy = unpack_weight(x_words, x_scales)[np.arange(K)[:, None], runs(hy, K)]
    h2 = 0.0625 * ((d_k3.T @ mxq(z, 0, "e4m3") + d_k4.T @ x_two + d_k5.T @ x_hy))
    pa2 = h2[np.arange(H)[:, None], runs(n6, H)]
    pb2 = h2[np.arange(H)[:, None], runs(n7, H)]
    rb2 = np.minimum(pa2, pb2)
    ra2 = np.maximum(pa2, pb2)
    ua2 = np.zeros((H, S))
    ua2[np.arange(H)[:, None], runs(n6, H)] = ra2
    ub2 = ua2.copy()
    ub2[np.arange(H)[:, None], runs(n7, H)] = rb2
    return ub2 - (ub2[np.arange(H)[:, None], runs(n8, H)])

@@ -1,0 +1,262 @@
+from contextlib import ExitStack
+
+import concourse.mybir as mybir
+from concourse.masks import make_identity
+
+K, T, S, G, H, W = 512, 1024, 512, 2048, 512, 256
+FLOPS = 5 * 2 * K * H * S
+
+F32 = mybir.dt.float32
+BF16 = mybir.dt.bfloat16
+I32 = mybir.dt.int32
+U32 = mybir.dt.uint32
+U16 = mybir.dt.uint16
+U8 = mybir.dt.uint8
+FP8X4 = mybir.dt.float8_e4m3fn_x4
+ALU = mybir.AluOpType
+COPY = mybir.ActivationFunctionType.Copy
+
+P = 128
+TILES = 4
+HALF = S // 2
+CHUNK = 8
+SIXTEENTH = 0.0625
+
+
+def tile_picked_mthzmthcpgfordd_none_p_kernel(
+    tc, x_words, x_scales, d_words, d_scales, gs, offs, k1, hz, k2, n1, n2, n3, n4, n5, k3, k4, two, k5, hy, n6, n7, n8, out
+):
+    nc = tc.nc
+    with ExitStack() as ctx:
+        held = ctx.enter_context(tc.tile_pool(name="held", bufs=1))
+        work = ctx.enter_context(tc.tile_pool(name="work", bufs=1))
+        psum = ctx.enter_context(tc.psum_pool(name="psum", bufs=1))
+
+        lists = {}
+
+        def load_list(name, src):
+            lists[name] = held.tile(list(src.shape), U16, name="list_" + name)
+            nc.sync.dma_start(lists[name][:], src)
+
+        def half_of(name, c):
+            return lists[name][:, c * (HALF // 16) : (c + 1) * (HALF // 16)]
+
+        d_bytes = work.tile([P, G], U8, name="d_bytes", align_bytes=64)
+        x_bytes = work.tile([P, T], U8, name="x_bytes", align_bytes=64)
+        nc.vector.memset(d_bytes[:].bitcast(I32), 0)
+        nc.vector.memset(x_bytes[:].bitcast(I32), 0)
+        for name, src in (("k1", k1), ("k2", k2), ("offs", offs), ("hz", hz)):
+            load_list(name, src)
+        nc.sync.dma_start(d_bytes[0:P:8, :].bitcast(I32), d_scales[0].bitcast(I32))
+        nc.sync.dma_start(x_bytes[0:P:8, :].bitcast(I32), x_scales[0].bitcast(I32))
+        x_tab = work.tile([P, T], I32, name="x_tab", align_bytes=64)
+        d_tab = work.tile([P, G], I32, name="d_tab", align_bytes=64)
+        nc.sync.dma_start(x_tab[:], x_words[0].rearrange("p n t -> p (n t)").bitcast(I32))
+        nc.sync.dma_start(d_tab[:], d_words[0].rearrange("p n t -> p (n t)").bitcast(I32))
+        for name, src in (
+            ("k4", k4), ("k5", k5), ("k3", k3), ("two", two), ("hy", hy), ("n1", n1), ("n2", n2),
+            ("n3", n3), ("n4", n4), ("n5", n5), ("n6", n6), ("n7", n7), ("n8", n8),
+        ):
+            load_list(name, src)
+        gain = work.tile([P, TILES], F32, name="gain")
+        nc.sync.dma_start(gain[:], gs.rearrange("(p t) o -> p (t o)", t=TILES))
+
+        ident = work.tile([P, P], F32, name="ident")
+        make_identity(nc, ident[:])
+
+        def zeroed_planes(name, width):
+            planes = work.tile([P, width], U8, name=name, align_bytes=64)
+            nc.vector.memset(planes[:].bitcast(I32), 0)
+            return planes
+
+        planes_1 = zeroed_planes("planes_1", 4 * S)
+        planes_d2 = zeroed_planes("planes_d2", 3 * H)
+        planes_x2 = zeroed_planes("planes_x2", 2 * S)
+
+        def gather_bytes(name, picks):
+            picked = work.tile([P, len(picks) * S], U8, name=name, align_bytes=64)
+            for i, (table, list_name) in enumerate(picks):
+                nc.vector.tensor_copy(picked[:, i * S : (i + 1) * S], table[:].indirect(lists[list_name][:]))
+            return picked
+
+        def place_rows(planes, picked):
+            for r in range(4):
+                nc.sync.dma_start(planes[r:P:32, :].bitcast(I32), picked[8 * r : P : 32, :].bitcast(I32))
+
+        def gather_words(table, list_name, tag=""):
+            picked = work.tile([P, S], U32, name="words_" + list_name, tag=tag or "words_" + list_name, align_bytes=64)
+            nc.vector.tensor_copy(picked[:], table[:].bitcast(U32).indirect(lists[list_name][:]))
+            return picked
+
+        def deal_words(picked, list_name):
+            dealt = work.tile([P, H], U32, name="dealt_" + list_name, align_bytes=64)
+            nc.vector.tensor_copy(
+                dealt[:].rearrange("p (t b q) -> p b t q", t=TILES, q=CHUNK),
+                picked[:].rearrange("p (b t q) -> p b t q", t=TILES, q=CHUNK),
+            )
+            return dealt
+
+        place_rows(planes_1, gather_bytes("bytes_1", ((d_bytes, "k1"), (d_bytes, "k2"), (x_bytes, "offs"), (x_bytes, "hz"))))
+        w_offs = gather_words(x_tab, "offs")
+        w_hz = gather_words(x_tab, "hz")
+        w_k1 = gather_words(d_tab, "k1")
+        w_k2 = gather_words(d_tab, "k2")
+        turned = []
+        for b in range(TILES):
+            cols = slice(b * P, (b + 1) * P)
+            bank = psum.tile([P, H], F32, name="sum_1", tag="sum%d" % b)
+            for i, (wx, wd) in enumerate(((w_offs, w_k1), (w_hz, w_k2))):
+                nc.tensor.matmul_mx(
+                    out=bank[:],
+                    lhsT=wx[:, cols].bitcast(FP8X4),
+                    lhsT_scale=planes_1[:, (2 + i) * S + b * P : (2 + i) * S + (b + 1) * P],
+                    rhs=wd[:].bitcast(FP8X4),
+                    rhs_scale=planes_1[:, i * S : (i + 1) * S],
+                    start=(i == 0),
+                    stop=(i == 1),
+                )
+            h_turned = work.tile([P, TILES, P], F32, name="h_turned%d" % b)
+            nc.scalar.activation(h_turned[:], bank[:].rearrange("p (m t) -> p t m", t=TILES), COPY, scale=SIXTEENTH)
+            turned.append(h_turned)
+
+        pa, npb = [], []
+        for t in range(TILES):
+            bank = psum.tile([P, S], F32, name="back", tag="back%d" % t)
+            for b in range(TILES):
+                nc.tensor.transpose(bank[:, b * P : (b + 1) * P], turned[b][:, t, :], ident[:])
+            h = work.tile([P, S], F32, name="h%d" % t)
+            nc.scalar.copy(h[:], bank[:])
+            pa.append(work.tile([P, W], F32, name="pa%d" % t))
+            npb.append(work.tile([P, W], F32, name="npb%d" % t))
+            nc.scalar.activation(pa[t][:], h[:].indirect(lists["n1"][:]), COPY)
+            nc.scalar.activation(npb[t][:], h[:].indirect(lists["n2"][:]), COPY, scale=-1.0)
+
+        bytes_d2 = gather_bytes("bytes_d2", ((d_bytes, "k4"), (d_bytes, "k5"), (d_bytes, "k3")))
+        place_rows(planes_x2, gather_bytes("bytes_x2", ((x_bytes, "two"), (x_bytes, "hy"))))
+        dealt_bytes = work.tile([P, 3 * H], U8, name="dealt_bytes", align_bytes=64)
+        nc.vector.tensor_copy(
+            dealt_bytes[:].bitcast(I32).rearrange("p (t a e w) -> p a t e w", t=TILES, e=2, w=2),
+            bytes_d2[:].bitcast(I32).rearrange("p (a e t w) -> p a t e w", t=TILES, e=2, w=2),
+        )
+        place_rows(planes_d2, dealt_bytes)
+        w_k4 = gather_words(d_tab, "k4")
+        w_two = gather_words(x_tab, "two")
+        w_k4 = deal_words(w_k4, "k4")
+        w_hy = gather_words(x_tab, "hy")
+
+        sums_2 = {}
+        for t in range(TILES):
+            for c, tag in enumerate(("sum%d", "back%d")):
+                sums_2[t, c] = psum.tile([P, HALF], F32, name="sum_2", tag=tag % t)
+
+        def second_pass(t, c, i, wd, wx, x_plane):
+            cols = slice(c * HALF, (c + 1) * HALF)
+            nc.tensor.matmul_mx(
+                out=sums_2[t, c][:],
+                lhsT=wd[:, t * P : (t + 1) * P].bitcast(FP8X4),
+                lhsT_scale=planes_d2[:, (3 * t + i) * P : (3 * t + i + 1) * P],
+                rhs=wx[:, cols].bitcast(FP8X4),
+                rhs_scale=x_plane[:, cols],
+                start=(i == 0),
+                stop=(i == 2),
+            )
+
+        for t in range(TILES):
+            for c in range(2):
+                second_pass(t, c, 0, w_k4, w_two[:], planes_x2[:, 0:S])
+
+        z = work.tile([P, S, TILES], BF16, name="z", align_bytes=64)
+        ub = {}
+        far = {}
+
+        def fetch_far(t):
+            for c in range(2):
+                far[t, c] = work.tile([P, HALF], F32, name="far", tag="far%d_%d" % (t, c), align_bytes=64)
+                nc.scalar.activation(far[t, c][:], ub[t][:].indirect(half_of("n5", c)), COPY)
+
+        def finish_z(t, c):
+            cols = slice(c * HALF, (c + 1) * HALF)
+            larger = work.tile([P, HALF], F32, name="larger", bufs=4)
+            nc.vector.tensor_tensor(larger[:], ub[t][:, cols], far[t, c][:], ALU.max)
+            nc.scalar.activation(z[:, cols, t], larger[:], COPY, scale=gain[:, t : t + 1])
+
+        for t in range(TILES):
+            ub[t] = work.tile([P, S], F32, name="ub", bufs=2)
+            nc.vector.tensor_tensor(ub[t][:].indirect(lists["n3"][:]), pa[t][:], npb[t][:], ALU.add)
+            if t > 0:
+                finish_z(t - 1, 0)
+            rb = work.tile([P, W], F32, name="rb", tag="far%d_0" % (t - 1), align_bytes=64)
+            nc.vector.scalar_tensor_tensor(rb[:], npb[t][:], -1.0, pa[t][:], ALU.mult, ALU.min)
+            if t > 0:
+                finish_z(t - 1, 1)
+            nc.vector.tensor_copy(ub[t][:].indirect(lists["n4"][:]), rb[:])
+            fetch_far(t)
+        last = TILES - 1
+        w_k5 = gather_words(d_tab, "k5", tag="far%d_0" % (last - 1))
+        finish_z(last, 0)
+        w_k5 = deal_words(w_k5, "k5")
+        finish_z(last, 1)
+        for t in range(TILES):
+            for c in range(2):
+                second_pass(t, c, 1, w_k5, w_hy[:], planes_x2[:, S : 2 * S])
+        w_k3 = deal_words(gather_words(d_tab, "k3", tag="far%d_1" % last), "k3")
+
+        z_words = work.tile([P, S], U32, name="z_words", align_bytes=64)
+        z_plane = work.tile([P, S], U8, name="z_plane", align_bytes=64)
+        for c in range(2):
+            cols = slice(c * HALF, (c + 1) * HALF)
+            nc.vector.quantize_mx(
+                out=z_words[:, cols].bitcast(FP8X4), scales=z_plane[:, cols], in_=z[:, cols, :].rearrange("p n t -> p (n t)")
+            )
+
+        pa2, pb2 = [], []
+        for t in range(TILES):
+            h2 = work.tile([P, S], F32, name="h2_%d" % t)
+            pa2.append(work.tile([P, W], F32, name="pa2_%d" % t))
+            pb2.append(work.tile([P, W], F32, name="pb2_%d" % t))
+            for c in range(2):
+                second_pass(t, c, 2, w_k3, z_words[:], z_plane[:])
+            nc.scalar.activation(h2[:, 0:HALF], sums_2[t, 0][:], COPY, scale=SIXTEENTH)
+            if t == 0:
+                nc.vector.tensor_scalar_mul(h2[:, HALF:S], sums_2[t, 1][:], SIXTEENTH)
+                nc.vector.tensor_copy(pa2[t][:], h2[:].indirect(lists["n6"][:]))
+            else:
+                nc.scalar.activation(h2[:, HALF:S], sums_2[t, 1][:], COPY, scale=SIXTEENTH)
+                nc.scalar.activation(pa2[t][:], h2[:].indirect(lists["n6"][:]), COPY)
+            nc.scalar.activation(pb2[t][:], h2[:].indirect(lists["n7"][:]), COPY)
+
+        out_rows = out.rearrange("(b t q) j -> t b q j", t=TILES, q=CHUNK)
+        ub2 = {}
+        far2 = {}
+        ra2 = {}
+
+        def larger_of_pair(t):
+            ra2[t] = work.tile([P, W], F32, name="ra2_%d" % t)
+            nc.vector.tensor_tensor(ra2[t][:], pa2[t][:], pb2[t][:], ALU.max)
+
+        def finish_out(t, c):
+            cols = slice(c * HALF, (c + 1) * HALF)
+            result = work.tile([P, HALF], F32, name="result", bufs=8)
+            nc.vector.tensor_tensor(result[:], ub2[t][:, cols], far2[t, c][:], ALU.subtract)
+            nc.sync.dma_start(out_rows[t][:, :, cols], result[:])
+
+        larger_of_pair(0)
+        for t in range(TILES):
+            ub2[t] = work.tile([P, S], F32, name="ub2", bufs=2)
+            if t == 0:
+                rb2 = work.tile([P, W], F32, name="rb2", tag="far2%d_0" % (t - 1))
+                nc.vector.tensor_tensor(rb2[:], pa2[t][:], pb2[t][:], ALU.min)
+            nc.vector.tensor_copy(ub2[t][:].indirect(lists["n6"][:]), ra2[t][:])
+            if t > 0:
+                finish_out(t - 1, 0)
+                rb2 = work.tile([P, W], F32, name="rb2", tag="far2%d_0" % (t - 1))
+                nc.vector.tensor_tensor(rb2[:], pa2[t][:], pb2[t][:], ALU.min)
+                finish_out(t - 1, 1)
+            if t < last:
+                larger_of_pair(t + 1)
+            nc.vector.tensor_copy(ub2[t][:].indirect(lists["n7"][:]), rb2[:])
+            for c in range(2):
+                far2[t, c] = work.tile([P, HALF], F32, name="far2", tag="far2%d_%d" % (t, c))
+                nc.scalar.activation(far2[t, c][:], ub2[t][:].indirect(half_of("n8", c)), COPY)
+        finish_out(last, 0)
+        finish_out(last, 1)

@@ -15,6 +15,7 @@ U8 = mybir.dt.uint8
 FP8X4 = mybir.dt.float8_e4m3fn_x4
 ALU = mybir.AluOpType
 COPY = mybir.ActivationFunctionType.Copy
+RELU = mybir.ActivationFunctionType.Relu
 
 P = 128
 TILES = 4
@@ -43,12 +44,12 @@ def tile_picked_mthzmthcpgfordd_none_p_kernel(
 
         d_bytes = work.tile([P, G], U8, name="d_bytes", align_bytes=64)
         x_bytes = work.tile([P, T], U8, name="x_bytes", align_bytes=64)
-        nc.vector.memset(d_bytes[:].bitcast(I32), 0)
-        nc.vector.memset(x_bytes[:].bitcast(I32), 0)
-        for name, src in (("k1", k1), ("k2", k2), ("offs", offs), ("hz", hz)):
-            load_list(name, src)
-        nc.sync.dma_start(d_bytes[0:P:8, :].bitcast(I32), d_scales[0].bitcast(I32))
-        nc.sync.dma_start(x_bytes[0:P:8, :].bitcast(I32), x_scales[0].bitcast(I32))
+        nc.sync.dma_start(x_bytes[:].bitcast(I32), x_scales[0].bitcast(I32).unsqueeze(1).to_broadcast([16, 8, T // 4]))
+        load_list("offs", offs)
+        load_list("hz", hz)
+        nc.sync.dma_start(d_bytes[:].bitcast(I32), d_scales[0].bitcast(I32).unsqueeze(1).to_broadcast([16, 8, G // 4]))
+        load_list("k1", k1)
+        load_list("k2", k2)
         x_tab = work.tile([P, T], I32, name="x_tab", align_bytes=64)
         d_tab = work.tile([P, G], I32, name="d_tab", align_bytes=64)
         nc.sync.dma_start(x_tab[:], x_words[0].rearrange("p n t -> p (n t)").bitcast(I32))
@@ -96,7 +97,7 @@ def tile_picked_mthzmthcpgfordd_none_p_kernel(
             )
             return dealt
 
-        place_rows(planes_1, gather_bytes("bytes_1", ((d_bytes, "k1"), (d_bytes, "k2"), (x_bytes, "offs"), (x_bytes, "hz"))))
+        place_rows(planes_1, gather_bytes("bytes_1", ((x_bytes, "offs"), (x_bytes, "hz"), (d_bytes, "k1"), (d_bytes, "k2"))))
         w_offs = gather_words(x_tab, "offs")
         w_hz = gather_words(x_tab, "hz")
         w_k1 = gather_words(d_tab, "k1")
@@ -109,9 +110,9 @@ def tile_picked_mthzmthcpgfordd_none_p_kernel(
                 nc.tensor.matmul_mx(
                     out=bank[:],
                     lhsT=wx[:, cols].bitcast(FP8X4),
-                    lhsT_scale=planes_1[:, (2 + i) * S + b * P : (2 + i) * S + (b + 1) * P],
+                    lhsT_scale=planes_1[:, i * S + b * P : i * S + (b + 1) * P],
                     rhs=wd[:].bitcast(FP8X4),
-                    rhs_scale=planes_1[:, i * S : (i + 1) * S],
+                    rhs_scale=planes_1[:, (2 + i) * S : (3 + i) * S],
                     start=(i == 0),
                     stop=(i == 1),
                 )
@@ -124,7 +125,7 @@ def tile_picked_mthzmthcpgfordd_none_p_kernel(
             bank = psum.tile([P, S], F32, name="back", tag="back%d" % t)
             for b in range(TILES):
                 nc.tensor.transpose(bank[:, b * P : (b + 1) * P], turned[b][:, t, :], ident[:])
-            h = work.tile([P, S], F32, name="h%d" % t)
+            h = work.tile([P, S], F32, name="h", tag="h%d" % t, align_bytes=64)
             nc.scalar.copy(h[:], bank[:])
             pa.append(work.tile([P, W], F32, name="pa%d" % t))
             npb.append(work.tile([P, W], F32, name="npb%d" % t))
@@ -180,26 +181,31 @@ def tile_picked_mthzmthcpgfordd_none_p_kernel(
             nc.vector.tensor_tensor(larger[:], ub[t][:, cols], far[t, c][:], ALU.max)
             nc.scalar.activation(z[:, cols, t], larger[:], COPY, scale=gain[:, t : t + 1])
 
+        rb = {}
+
+        def smaller_of_pair(t):
+            rb[t] = work.tile([P, W], F32, name="rb", tag="far%d_1" % (t - 3), align_bytes=64)
+            nc.vector.scalar_tensor_tensor(rb[t][:], npb[t][:], -1.0, pa[t][:], ALU.mult, ALU.min)
+
+        last = TILES - 1
+        smaller_of_pair(0)
         for t in range(TILES):
-            ub[t] = work.tile([P, S], F32, name="ub", bufs=2)
+            ub[t] = work.tile([P, S], F32, name="ub", tag="h1" if t == 0 else "far%d_0" % (t - 2), align_bytes=64)
             nc.vector.tensor_tensor(ub[t][:].indirect(lists["n3"][:]), pa[t][:], npb[t][:], ALU.add)
+            if t < last:
+                smaller_of_pair(t + 1)
+            nc.vector.tensor_copy(ub[t][:].indirect(lists["n4"][:]), rb[t][:])
+            fetch_far(t)
             if t > 0:
                 finish_z(t - 1, 0)
-            rb = work.tile([P, W], F32, name="rb", tag="far%d_0" % (t - 1), align_bytes=64)
-            nc.vector.scalar_tensor_tensor(rb[:], npb[t][:], -1.0, pa[t][:], ALU.mult, ALU.min)
-            if t > 0:
                 finish_z(t - 1, 1)
-            nc.vector.tensor_copy(ub[t][:].indirect(lists["n4"][:]), rb[:])
-            fetch_far(t)
-        last = TILES - 1
-        w_k5 = gather_words(d_tab, "k5", tag="far%d_0" % (last - 1))
         finish_z(last, 0)
-        w_k5 = deal_words(w_k5, "k5")
         finish_z(last, 1)
+        w_k5 = deal_words(gather_words(d_tab, "k5", tag="far%d_1" % (last - 3)), "k5")
         for t in range(TILES):
             for c in range(2):
                 second_pass(t, c, 1, w_k5, w_hy[:], planes_x2[:, S : 2 * S])
-        w_k3 = deal_words(gather_words(d_tab, "k3", tag="far%d_1" % last), "k3")
+        w_k3 = deal_words(gather_words(d_tab, "k3", tag="far%d_1" % (last - 1)), "k3")
 
         z_words = work.tile([P, S], U32, name="z_words", align_bytes=64)
         z_plane = work.tile([P, S], U8, name="z_plane", align_bytes=64)
@@ -230,33 +236,35 @@ def tile_picked_mthzmthcpgfordd_none_p_kernel(
         far2 = {}
         ra2 = {}
 
-        def larger_of_pair(t):
+        rb2 = {}
+
+        def order_pairs(t):
             ra2[t] = work.tile([P, W], F32, name="ra2_%d" % t)
-            nc.vector.tensor_tensor(ra2[t][:], pa2[t][:], pb2[t][:], ALU.max)
-
-        def finish_out(t, c):
-            cols = slice(c * HALF, (c + 1) * HALF)
-            result = work.tile([P, HALF], F32, name="result", bufs=8)
-            nc.vector.tensor_tensor(result[:], ub2[t][:, cols], far2[t, c][:], ALU.subtract)
-            nc.sync.dma_start(out_rows[t][:, :, cols], result[:])
-
-        larger_of_pair(0)
-        for t in range(TILES):
-            ub2[t] = work.tile([P, S], F32, name="ub2", bufs=2)
+            rb2[t] = work.tile([P, W], F32, name="rb2_%d" % t)
+            nc.vector.tensor_tensor(rb2[t][:], pa2[t][:], pb2[t][:], ALU.min)
             if t == 0:
-                rb2 = work.tile([P, W], F32, name="rb2", tag="far2%d_0" % (t - 1))
-                nc.vector.tensor_tensor(rb2[:], pa2[t][:], pb2[t][:], ALU.min)
+                nc.vector.tensor_tensor(ra2[t][:], pa2[t][:], pb2[t][:], ALU.max)
+            else:
+                lead = work.tile([P, W], F32, name="lead%d" % t)
+                excess = work.tile([P, W], F32, name="excess%d" % t)
+                nc.gpsimd.tensor_tensor(lead[:], pb2[t][:], pa2[t][:], ALU.subtract)
+                nc.scalar.activation(excess[:], lead[:], RELU)
+                nc.gpsimd.tensor_tensor(ra2[t][:], pa2[t][:], excess[:], ALU.add)
+
+        for t in range(TILES):
+            order_pairs(t)
+        for t in range(TILES):
+            ub2[t] = work.tile([P, S], F32, name="ub2_%d" % t)
+            nc.vector.tensor_copy(ub2[t][:].indirect(lists["n7"][:]), rb2[t][:])
             nc.vector.tensor_copy(ub2[t][:].indirect(lists["n6"][:]), ra2[t][:])
-            if t > 0:
-                finish_out(t - 1, 0)
-                rb2 = work.tile([P, W], F32, name="rb2", tag="far2%d_0" % (t - 1))
-                nc.vector.tensor_tensor(rb2[:], pa2[t][:], pb2[t][:], ALU.min)
-                finish_out(t - 1, 1)
-            if t < last:
-                larger_of_pair(t + 1)
-            nc.vector.tensor_copy(ub2[t][:].indirect(lists["n7"][:]), rb2[:])
+            far2[t] = work.tile([P, S], F32, name="other%d" % t)
+            result = work.tile([P, S], F32, name="result%d" % t)
             for c in range(2):
-                far2[t, c] = work.tile([P, HALF], F32, name="far2", tag="far2%d_%d" % (t, c))
-                nc.scalar.activation(far2[t, c][:], ub2[t][:].indirect(half_of("n8", c)), COPY)
-        finish_out(last, 0)
-        finish_out(last, 1)
+                cols = slice(c * HALF, (c + 1) * HALF)
+                nc.scalar.activation(far2[t][:, cols], ub2[t][:].indirect(half_of("n8", c)), COPY)
+                if t == last:
+                    nc.vector.tensor_tensor(result[:, cols], ub2[t][:, cols], far2[t][:, cols], ALU.subtract)
+                    nc.sync.dma_start(out_rows[t][:, :, cols], result[:, cols])
+            if t < last:
+                nc.gpsimd.tensor_tensor(result[:], ub2[t][:], far2[t][:], ALU.subtract)
+                nc.sync.dma_start(out_rows[t], result[:])

@@ -59,10 +59,10 @@ def tile_picked_mthzmthcpgfordd_none_p_kernel(
             ("n3", n3), ("n4", n4), ("n5", n5), ("n6", n6), ("n7", n7), ("n8", n8),
         ):
             load_list(name, src)
-        gain = work.tile([P, TILES], F32, name="gain")
+        gain = work.tile([P, TILES], F32, align_bytes=64, name="gain")
         nc.sync.dma_start(gain[:], gs.rearrange("(p t) o -> p (t o)", t=TILES))
 
-        ident = work.tile([P, P], F32, name="ident")
+        ident = work.tile([P, P], F32, align_bytes=64, name="ident")
         make_identity(nc, ident[:])
 
         def zeroed_planes(name, width):
@@ -99,8 +99,8 @@ def tile_picked_mthzmthcpgfordd_none_p_kernel(
 
         place_rows(planes_1, gather_bytes("bytes_1", ((x_bytes, "offs"), (x_bytes, "hz"), (d_bytes, "k1"), (d_bytes, "k2"))))
         w_offs = gather_words(x_tab, "offs")
-        w_hz = gather_words(x_tab, "hz")
         w_k1 = gather_words(d_tab, "k1")
+        w_hz = gather_words(x_tab, "hz")
         w_k2 = gather_words(d_tab, "k2")
         turned = []
         for b in range(TILES):
@@ -116,33 +116,43 @@ def tile_picked_mthzmthcpgfordd_none_p_kernel(
                     start=(i == 0),
                     stop=(i == 1),
                 )
-            h_turned = work.tile([P, TILES, P], F32, name="h_turned%d" % b)
+            h_turned = work.tile([P, TILES, P], F32, align_bytes=64, name="h_turned%d" % b)
             nc.scalar.activation(h_turned[:], bank[:].rearrange("p (m t) -> p t m", t=TILES), COPY, scale=SIXTEENTH)
             turned.append(h_turned)
 
-        pa, npb = [], []
+        def excess_over(name, lead):
+            excess = work.tile(list(lead.shape), F32, align_bytes=64, name=name)
+            nc.scalar.activation(excess[:], lead, RELU)
+            return excess
+
+        pa, ra, rb = [], [], []
         for t in range(TILES):
             bank = psum.tile([P, S], F32, name="back", tag="back%d" % t)
             for b in range(TILES):
                 nc.tensor.transpose(bank[:, b * P : (b + 1) * P], turned[b][:, t, :], ident[:])
-            h = work.tile([P, S], F32, name="h", tag="h%d" % t, align_bytes=64)
+            h = work.tile([P, S], F32, align_bytes=64, name="h%d" % t)
             nc.scalar.copy(h[:], bank[:])
-            pa.append(work.tile([P, W], F32, name="pa%d" % t))
-            npb.append(work.tile([P, W], F32, name="npb%d" % t))
+            pa.append(work.tile([P, W], F32, align_bytes=64, name="pa%d" % t))
+            pb = work.tile([P, W], F32, name="pb%d" % t, align_bytes=64)
             nc.scalar.activation(pa[t][:], h[:].indirect(lists["n1"][:]), COPY)
-            nc.scalar.activation(npb[t][:], h[:].indirect(lists["n2"][:]), COPY, scale=-1.0)
+            nc.scalar.activation(pb[:], h[:].indirect(lists["n2"][:]), COPY)
+            ra.append(work.tile([P, W], F32, align_bytes=64, name="ra%d" % t))
+            nc.gpsimd.tensor_tensor(ra[t][:], pa[t][:], pb[:], ALU.subtract)
+            excess = excess_over("excess_1_%d" % t, ra[t][:])
+            rb.append(work.tile([P, W], F32, name="rb%d" % t, align_bytes=64))
+            nc.gpsimd.tensor_tensor(rb[t][:], pa[t][:], excess[:], ALU.subtract)
 
         bytes_d2 = gather_bytes("bytes_d2", ((d_bytes, "k4"), (d_bytes, "k5"), (d_bytes, "k3")))
-        place_rows(planes_x2, gather_bytes("bytes_x2", ((x_bytes, "two"), (x_bytes, "hy"))))
+        w_k4 = gather_words(d_tab, "k4")
         dealt_bytes = work.tile([P, 3 * H], U8, name="dealt_bytes", align_bytes=64)
         nc.vector.tensor_copy(
             dealt_bytes[:].bitcast(I32).rearrange("p (t a e w) -> p a t e w", t=TILES, e=2, w=2),
             bytes_d2[:].bitcast(I32).rearrange("p (a e t w) -> p a t e w", t=TILES, e=2, w=2),
         )
         place_rows(planes_d2, dealt_bytes)
-        w_k4 = gather_words(d_tab, "k4")
-        w_two = gather_words(x_tab, "two")
         w_k4 = deal_words(w_k4, "k4")
+        place_rows(planes_x2, gather_bytes("bytes_x2", ((x_bytes, "two"), (x_bytes, "hy"))))
+        w_two = gather_words(x_tab, "two")
         w_hy = gather_words(x_tab, "hy")
 
         sums_2 = {}
@@ -166,42 +176,30 @@ def tile_picked_mthzmthcpgfordd_none_p_kernel(
             for c in range(2):
                 second_pass(t, c, 0, w_k4, w_two[:], planes_x2[:, 0:S])
 
+        last = TILES - 1
         z = work.tile([P, S, TILES], BF16, name="z", align_bytes=64)
         ub = {}
         far = {}
+        far_tags = {(0, 0): "h3", (0, 1): "pb3", (1, 0): "excess_1_3", (1, 1): "pa3"}
 
-        def fetch_far(t):
+        def finish_z(t):
             for c in range(2):
-                far[t, c] = work.tile([P, HALF], F32, name="far", tag="far%d_%d" % (t, c), align_bytes=64)
-                nc.scalar.activation(far[t, c][:], ub[t][:].indirect(half_of("n5", c)), COPY)
+                cols = slice(c * HALF, (c + 1) * HALF)
+                larger = work.tile([P, HALF], F32, align_bytes=64, name="larger", bufs=4)
+                nc.vector.tensor_tensor(larger[:], ub[t][:, cols], far[t, c][:], ALU.max)
+                nc.scalar.activation(z[:, cols, t], larger[:], COPY, scale=gain[:, t : t + 1])
 
-        def finish_z(t, c):
-            cols = slice(c * HALF, (c + 1) * HALF)
-            larger = work.tile([P, HALF], F32, name="larger", bufs=4)
-            nc.vector.tensor_tensor(larger[:], ub[t][:, cols], far[t, c][:], ALU.max)
-            nc.scalar.activation(z[:, cols, t], larger[:], COPY, scale=gain[:, t : t + 1])
-
-        rb = {}
-
-        def smaller_of_pair(t):
-            rb[t] = work.tile([P, W], F32, name="rb", tag="far%d_1" % (t - 3), align_bytes=64)
-            nc.vector.scalar_tensor_tensor(rb[t][:], npb[t][:], -1.0, pa[t][:], ALU.mult, ALU.min)
-
-        last = TILES - 1
-        smaller_of_pair(0)
         for t in range(TILES):
-            ub[t] = work.tile([P, S], F32, name="ub", tag="h1" if t == 0 else "far%d_0" % (t - 2), align_bytes=64)
-            nc.vector.tensor_tensor(ub[t][:].indirect(lists["n3"][:]), pa[t][:], npb[t][:], ALU.add)
-            if t < last:
-                smaller_of_pair(t + 1)
+            ub[t] = work.tile([P, S], F32, name="ub", tag=("pb1", "ub1", "h3", "excess_1_3")[t], align_bytes=64)
+            nc.vector.tensor_copy(ub[t][:].indirect(lists["n3"][:]), ra[t][:])
             nc.vector.tensor_copy(ub[t][:].indirect(lists["n4"][:]), rb[t][:])
-            fetch_far(t)
+            for c in range(2):
+                far[t, c] = work.tile([P, HALF], F32, name="far", tag=far_tags.get((t, c), "far%d_%d" % (t, c)), align_bytes=64)
+                nc.scalar.activation(far[t, c][:], ub[t][:].indirect(half_of("n5", c)), COPY)
             if t > 0:
-                finish_z(t - 1, 0)
-                finish_z(t - 1, 1)
-        finish_z(last, 0)
-        finish_z(last, 1)
-        w_k5 = deal_words(gather_words(d_tab, "k5", tag="far%d_1" % (last - 3)), "k5")
+                finish_z(t - 1)
+        finish_z(last)
+        w_k5 = deal_words(gather_words(d_tab, "k5", tag="rb%d" % last), "k5")
         for t in range(TILES):
             for c in range(2):
                 second_pass(t, c, 1, w_k5, w_hy[:], planes_x2[:, S : 2 * S])
@@ -215,11 +213,11 @@ def tile_picked_mthzmthcpgfordd_none_p_kernel(
                 out=z_words[:, cols].bitcast(FP8X4), scales=z_plane[:, cols], in_=z[:, cols, :].rearrange("p n t -> p (n t)")
             )
 
-        pa2, pb2 = [], []
+        pa2, pb2, ra2, rb2, excess_2 = [], [], [], [], {}
         for t in range(TILES):
-            h2 = work.tile([P, S], F32, name="h2_%d" % t)
-            pa2.append(work.tile([P, W], F32, name="pa2_%d" % t))
-            pb2.append(work.tile([P, W], F32, name="pb2_%d" % t))
+            h2 = work.tile([P, S], F32, align_bytes=64, name="h2_%d" % t)
+            pa2.append(work.tile([P, W], F32, align_bytes=64, name="pa2_%d" % t))
+            pb2.append(work.tile([P, W], F32, align_bytes=64, name="pb2_%d" % t))
             for c in range(2):
                 second_pass(t, c, 2, w_k3, z_words[:], z_plane[:])
             nc.scalar.activation(h2[:, 0:HALF], sums_2[t, 0][:], COPY, scale=SIXTEENTH)
@@ -230,41 +228,39 @@ def tile_picked_mthzmthcpgfordd_none_p_kernel(
                 nc.scalar.activation(h2[:, HALF:S], sums_2[t, 1][:], COPY, scale=SIXTEENTH)
                 nc.scalar.activation(pa2[t][:], h2[:].indirect(lists["n6"][:]), COPY)
             nc.scalar.activation(pb2[t][:], h2[:].indirect(lists["n7"][:]), COPY)
-
-        out_rows = out.rearrange("(b t q) j -> t b q j", t=TILES, q=CHUNK)
-        ub2 = {}
-        far2 = {}
-        ra2 = {}
-
-        rb2 = {}
-
-        def order_pairs(t):
-            ra2[t] = work.tile([P, W], F32, name="ra2_%d" % t)
-            rb2[t] = work.tile([P, W], F32, name="rb2_%d" % t)
-            nc.vector.tensor_tensor(rb2[t][:], pa2[t][:], pb2[t][:], ALU.min)
-            if t == 0:
+            rb2.append(work.tile([P, W], F32, align_bytes=64, name="rb2_%d" % t))
+            if t < 2:
+                nc.vector.tensor_tensor(rb2[t][:], pa2[t][:], pb2[t][:], ALU.min)
+            else:
+                lead = work.tile([P, W], F32, align_bytes=64, name="lead%d" % t)
+                nc.gpsimd.tensor_tensor(lead[:], pb2[t][:], pa2[t][:], ALU.subtract)
+                excess_2[t] = excess_over("excess_2_%d" % t, lead[:])
+                nc.gpsimd.tensor_tensor(rb2[t][:], pb2[t][:], excess_2[t][:], ALU.subtract)
+        for t in range(TILES):
+            ra2.append(work.tile([P, W], F32, align_bytes=64, name="ra2", tag=("h2_1", "ra2_1", "lead3", "ra2_3")[t]))
+            if t < 2:
                 nc.vector.tensor_tensor(ra2[t][:], pa2[t][:], pb2[t][:], ALU.max)
             else:
-                lead = work.tile([P, W], F32, name="lead%d" % t)
-                excess = work.tile([P, W], F32, name="excess%d" % t)
-                nc.gpsimd.tensor_tensor(lead[:], pb2[t][:], pa2[t][:], ALU.subtract)
-                nc.scalar.activation(excess[:], lead[:], RELU)
-                nc.gpsimd.tensor_tensor(ra2[t][:], pa2[t][:], excess[:], ALU.add)
+                nc.gpsimd.tensor_tensor(ra2[t][:], pa2[t][:], excess_2[t][:], ALU.add)
 
+        out_rows = out.rearrange("(b t q) j -> t b q j", t=TILES, q=CHUNK)
+        ub2 = [work.tile([P, S], F32, align_bytes=64, name="ub2_%d" % t) for t in range(TILES)]
+        for pair in ((0, 1), (2, 3)):
+            for t in pair:
+                nc.vector.tensor_copy(ub2[t][:].indirect(lists["n7"][:]), rb2[t][:])
+            for t in pair:
+                nc.vector.tensor_copy(ub2[t][:].indirect(lists["n6"][:]), ra2[t][:])
         for t in range(TILES):
-            order_pairs(t)
-        for t in range(TILES):
-            ub2[t] = work.tile([P, S], F32, name="ub2_%d" % t)
-            nc.vector.tensor_copy(ub2[t][:].indirect(lists["n7"][:]), rb2[t][:])
-            nc.vector.tensor_copy(ub2[t][:].indirect(lists["n6"][:]), ra2[t][:])
-            far2[t] = work.tile([P, S], F32, name="other%d" % t)
-            result = work.tile([P, S], F32, name="result%d" % t)
-            for c in range(2):
-                cols = slice(c * HALF, (c + 1) * HALF)
-                nc.scalar.activation(far2[t][:, cols], ub2[t][:].indirect(half_of("n8", c)), COPY)
+            other = work.tile([P, S], F32, align_bytes=64, name="other", tag=("pb2_3", "excess_2_2", "other2", "other3")[t])
+            result = work.tile([P, S], F32, align_bytes=64, name="result", tag=("excess_2_3", "pa2_3", "ra2_3", "result3")[t])
+            cuts = (0, HALF, S - P, S) if t == last else (0, HALF, S)
+            for lo, hi in zip(cuts, cuts[1:]):
+                cols = slice(lo, hi)
+                nc.scalar.activation(other[:, cols], ub2[t][:].indirect(lists["n8"][:, lo // 16 : hi // 16]), COPY)
                 if t == last:
-                    nc.vector.tensor_tensor(result[:, cols], ub2[t][:, cols], far2[t][:, cols], ALU.subtract)
+                    nc.vector.tensor_tensor(result[:, cols], ub2[t][:, cols], other[:, cols], ALU.subtract)
                     nc.sync.dma_start(out_rows[t][:, :, cols], result[:, cols])
             if t < last:
-                nc.gpsimd.tensor_tensor(result[:], ub2[t][:], far2[t][:], ALU.subtract)
+                engine = nc.gpsimd if t < 2 else nc.vector
+                engine.tensor_tensor(result[:], ub2[t][:], other[:], ALU.subtract)
                 nc.sync.dma_start(out_rows[t], result[:])

@@ -117,7 +117,12 @@ def tile_picked_mthzmthcpgfordd_none_p_kernel(
                     stop=(i == 1),
                 )
             h_turned = work.tile([P, TILES, P], F32, align_bytes=64, name="h_turned%d" % b)
-            nc.scalar.activation(h_turned[:], bank[:].rearrange("p (m t) -> p t m", t=TILES), COPY, scale=SIXTEENTH)
+            nc.scalar.activation(
+                h_turned[:].rearrange("p t (m i) -> p m t i", i=4),
+                bank[:].rearrange("p (m i t) -> p m t i", i=4, t=TILES),
+                COPY,
+                scale=SIXTEENTH,
+            )
             turned.append(h_turned)
 
         def excess_over(name, lead):
@@ -130,7 +135,7 @@ def tile_picked_mthzmthcpgfordd_none_p_kernel(
             bank = psum.tile([P, S], F32, name="back", tag="back%d" % t)
             for b in range(TILES):
                 nc.tensor.transpose(bank[:, b * P : (b + 1) * P], turned[b][:, t, :], ident[:])
-            h = work.tile([P, S], F32, align_bytes=64, name="h%d" % t)
+            h = work.tile([P, S], F32, align_bytes=64, name="h", tag="h%d" % (t % 2))
             nc.scalar.copy(h[:], bank[:])
             pa.append(work.tile([P, W], F32, align_bytes=64, name="pa%d" % t))
             pb = work.tile([P, W], F32, name="pb%d" % t, align_bytes=64)
@@ -153,7 +158,6 @@ def tile_picked_mthzmthcpgfordd_none_p_kernel(
         w_k4 = deal_words(w_k4, "k4")
         place_rows(planes_x2, gather_bytes("bytes_x2", ((x_bytes, "two"), (x_bytes, "hy"))))
         w_two = gather_words(x_tab, "two")
-        w_hy = gather_words(x_tab, "hy")
 
         sums_2 = {}
         for t in range(TILES):
@@ -180,7 +184,7 @@ def tile_picked_mthzmthcpgfordd_none_p_kernel(
         z = work.tile([P, S, TILES], BF16, name="z", align_bytes=64)
         ub = {}
         far = {}
-        far_tags = {(0, 0): "h3", (0, 1): "pb3", (1, 0): "excess_1_3", (1, 1): "pa3"}
+        far_tags = {(0, 0): "h1", (0, 1): "pb3", (1, 0): "excess_1_3", (1, 1): "pa3"}
 
         def finish_z(t):
             for c in range(2):
@@ -190,7 +194,7 @@ def tile_picked_mthzmthcpgfordd_none_p_kernel(
                 nc.scalar.activation(z[:, cols, t], larger[:], COPY, scale=gain[:, t : t + 1])
 
         for t in range(TILES):
-            ub[t] = work.tile([P, S], F32, name="ub", tag=("pb1", "ub1", "h3", "excess_1_3")[t], align_bytes=64)
+            ub[t] = work.tile([P, S], F32, name="ub", tag=("pb1", "ub1", "h1", "excess_1_3")[t], align_bytes=64)
             nc.vector.tensor_copy(ub[t][:].indirect(lists["n3"][:]), ra[t][:])
             nc.vector.tensor_copy(ub[t][:].indirect(lists["n4"][:]), rb[t][:])
             for c in range(2):
@@ -199,11 +203,13 @@ def tile_picked_mthzmthcpgfordd_none_p_kernel(
             if t > 0:
                 finish_z(t - 1)
         finish_z(last)
-        w_k5 = deal_words(gather_words(d_tab, "k5", tag="rb%d" % last), "k5")
+        w_k5 = gather_words(d_tab, "k5", tag="far%d_1" % (last - 1))
+        w_hy = gather_words(x_tab, "hy", tag="rb%d" % last)
+        w_k5 = deal_words(w_k5, "k5")
         for t in range(TILES):
             for c in range(2):
                 second_pass(t, c, 1, w_k5, w_hy[:], planes_x2[:, S : 2 * S])
-        w_k3 = deal_words(gather_words(d_tab, "k3", tag="far%d_1" % (last - 1)), "k3")
+        w_k3 = deal_words(gather_words(d_tab, "k3", tag="far%d_1" % last), "k3")
 
         z_words = work.tile([P, S], U32, name="z_words", align_bytes=64)
         z_plane = work.tile([P, S], U8, name="z_plane", align_bytes=64)

from contextlib import ExitStack

import concourse.mybir as mybir
from concourse.masks import make_identity

K, T, S, G, H, W = 512, 1024, 512, 2048, 512, 256
FLOPS = 5 * 2 * K * H * S

F32 = mybir.dt.float32
BF16 = mybir.dt.bfloat16
I32 = mybir.dt.int32
U32 = mybir.dt.uint32
U16 = mybir.dt.uint16
U8 = mybir.dt.uint8
FP8X4 = mybir.dt.float8_e4m3fn_x4
ALU = mybir.AluOpType
COPY = mybir.ActivationFunctionType.Copy
RELU = mybir.ActivationFunctionType.Relu

P = 128
TILES = 4
HALF = S // 2
CHUNK = 8
SIXTEENTH = 0.0625


def tile_picked_mthzmthcpgfordd_none_p_kernel(
    tc, x_words, x_scales, d_words, d_scales, gs, offs, k1, hz, k2, n1, n2, n3, n4, n5, k3, k4, two, k5, hy, n6, n7, n8, out
):
    nc = tc.nc
    with ExitStack() as ctx:
        held = ctx.enter_context(tc.tile_pool(name="held", bufs=1))
        work = ctx.enter_context(tc.tile_pool(name="work", bufs=1))
        psum = ctx.enter_context(tc.psum_pool(name="psum", bufs=1))

        lists = {}

        def load_list(name, src):
            lists[name] = held.tile(list(src.shape), U16, name="list_" + name)
            nc.sync.dma_start(lists[name][:], src)

        def half_of(name, c):
            return lists[name][:, c * (HALF // 16) : (c + 1) * (HALF // 16)]

        d_bytes = work.tile([P, G], U8, name="d_bytes", align_bytes=64)
        x_bytes = work.tile([P, T], U8, name="x_bytes", align_bytes=64)
        nc.sync.dma_start(x_bytes[:].bitcast(I32), x_scales[0].bitcast(I32).unsqueeze(1).to_broadcast([16, 8, T // 4]))
        load_list("offs", offs)
        load_list("hz", hz)
        nc.sync.dma_start(d_bytes[:].bitcast(I32), d_scales[0].bitcast(I32).unsqueeze(1).to_broadcast([16, 8, G // 4]))
        load_list("k1", k1)
        load_list("k2", k2)
        x_tab = work.tile([P, T], I32, name="x_tab", align_bytes=64)
        d_tab = work.tile([P, G], I32, name="d_tab", align_bytes=64)
        nc.sync.dma_start(x_tab[:], x_words[0].rearrange("p n t -> p (n t)").bitcast(I32))
        nc.sync.dma_start(d_tab[:], d_words[0].rearrange("p n t -> p (n t)").bitcast(I32))
        for name, src in (
            ("k4", k4), ("k5", k5), ("k3", k3), ("two", two), ("hy", hy), ("n1", n1), ("n2", n2),
            ("n3", n3), ("n4", n4), ("n5", n5), ("n6", n6), ("n7", n7), ("n8", n8),
        ):
            load_list(name, src)
        gain = work.tile([P, TILES], F32, align_bytes=64, name="gain")
        nc.sync.dma_start(gain[:], gs.rearrange("(p t) o -> p (t o)", t=TILES))

        ident = work.tile([P, P], F32, align_bytes=64, name="ident")
        make_identity(nc, ident[:])

        def zeroed_planes(name, width):
            planes = work.tile([P, width], U8, name=name, align_bytes=64)
            nc.vector.memset(planes[:].bitcast(I32), 0)
            return planes

        planes_1 = zeroed_planes("planes_1", 4 * S)
        planes_d2 = zeroed_planes("planes_d2", 3 * H)
        planes_x2 = zeroed_planes("planes_x2", 2 * S)

        def gather_bytes(name, picks):
            picked = work.tile([P, len(picks) * S], U8, name=name, align_bytes=64)
            for i, (table, list_name) in enumerate(picks):
                nc.vector.tensor_copy(picked[:, i * S : (i + 1) * S], table[:].indirect(lists[list_name][:]))
            return picked

        def place_rows(planes, picked):
            for r in range(4):
                nc.sync.dma_start(planes[r:P:32, :].bitcast(I32), picked[8 * r : P : 32, :].bitcast(I32))

        def gather_words(table, list_name, tag=""):
            picked = work.tile([P, S], U32, name="words_" + list_name, tag=tag or "words_" + list_name, align_bytes=64)
            nc.vector.tensor_copy(picked[:], table[:].bitcast(U32).indirect(lists[list_name][:]))
            return picked

        def deal_words(picked, list_name):
            dealt = work.tile([P, H], U32, name="dealt_" + list_name, align_bytes=64)
            nc.vector.tensor_copy(
                dealt[:].rearrange("p (t b q) -> p b t q", t=TILES, q=CHUNK),
                picked[:].rearrange("p (b t q) -> p b t q", t=TILES, q=CHUNK),
            )
            return dealt

        place_rows(planes_1, gather_bytes("bytes_1", ((x_bytes, "offs"), (x_bytes, "hz"), (d_bytes, "k1"), (d_bytes, "k2"))))
        w_offs = gather_words(x_tab, "offs")
        w_k1 = gather_words(d_tab, "k1")
        w_hz = gather_words(x_tab, "hz")
        w_k2 = gather_words(d_tab, "k2")
        turned = []
        for b in range(TILES):
            cols = slice(b * P, (b + 1) * P)
            bank = psum.tile([P, H], F32, name="sum_1", tag="sum%d" % b)
            for i, (wx, wd) in enumerate(((w_offs, w_k1), (w_hz, w_k2))):
                nc.tensor.matmul_mx(
                    out=bank[:],
                    lhsT=wx[:, cols].bitcast(FP8X4),
                    lhsT_scale=planes_1[:, i * S + b * P : i * S + (b + 1) * P],
                    rhs=wd[:].bitcast(FP8X4),
                    rhs_scale=planes_1[:, (2 + i) * S : (3 + i) * S],
                    start=(i == 0),
                    stop=(i == 1),
                )
            h_turned = work.tile([P, TILES, P], F32, align_bytes=64, name="h_turned%d" % b)
            nc.scalar.activation(
                h_turned[:].rearrange("p t (m i) -> p m t i", i=4),
                bank[:].rearrange("p (m i t) -> p m t i", i=4, t=TILES),
                COPY,
                scale=SIXTEENTH,
            )
            turned.append(h_turned)

        def excess_over(name, lead):
            excess = work.tile(list(lead.shape), F32, align_bytes=64, name=name)
            nc.scalar.activation(excess[:], lead, RELU)
            return excess

        pa, ra, rb = [], [], []
        for t in range(TILES):
            bank = psum.tile([P, S], F32, name="back", tag="back%d" % t)
            for b in range(TILES):
                nc.tensor.transpose(bank[:, b * P : (b + 1) * P], turned[b][:, t, :], ident[:])
            h = work.tile([P, S], F32, align_bytes=64, name="h", tag="h%d" % (t % 2))
            nc.scalar.copy(h[:], bank[:])
            pa.append(work.tile([P, W], F32, align_bytes=64, name="pa%d" % t))
            pb = work.tile([P, W], F32, name="pb%d" % t, align_bytes=64)
            nc.scalar.activation(pa[t][:], h[:].indirect(lists["n1"][:]), COPY)
            nc.scalar.activation(pb[:], h[:].indirect(lists["n2"][:]), COPY)
            ra.append(work.tile([P, W], F32, align_bytes=64, name="ra%d" % t))
            nc.gpsimd.tensor_tensor(ra[t][:], pa[t][:], pb[:], ALU.subtract)
            excess = excess_over("excess_1_%d" % t, ra[t][:])
            rb.append(work.tile([P, W], F32, name="rb%d" % t, align_bytes=64))
            nc.gpsimd.tensor_tensor(rb[t][:], pa[t][:], excess[:], ALU.subtract)

        bytes_d2 = gather_bytes("bytes_d2", ((d_bytes, "k4"), (d_bytes, "k5"), (d_bytes, "k3")))
        w_k4 = gather_words(d_tab, "k4")
        dealt_bytes = work.tile([P, 3 * H], U8, name="dealt_bytes", align_bytes=64)
        nc.vector.tensor_copy(
            dealt_bytes[:].bitcast(I32).rearrange("p (t a e w) -> p a t e w", t=TILES, e=2, w=2),
            bytes_d2[:].bitcast(I32).rearrange("p (a e t w) -> p a t e w", t=TILES, e=2, w=2),
        )
        place_rows(planes_d2, dealt_bytes)
        w_k4 = deal_words(w_k4, "k4")
        place_rows(planes_x2, gather_bytes("bytes_x2", ((x_bytes, "two"), (x_bytes, "hy"))))
        w_two = gather_words(x_tab, "two")

        sums_2 = {}
        for t in range(TILES):
            for c, tag in enumerate(("sum%d", "back%d")):
                sums_2[t, c] = psum.tile([P, HALF], F32, name="sum_2", tag=tag % t)

        def second_pass(t, c, i, wd, wx, x_plane):
            cols = slice(c * HALF, (c + 1) * HALF)
            nc.tensor.matmul_mx(
                out=sums_2[t, c][:],
                lhsT=wd[:, t * P : (t + 1) * P].bitcast(FP8X4),
                lhsT_scale=planes_d2[:, (3 * t + i) * P : (3 * t + i + 1) * P],
                rhs=wx[:, cols].bitcast(FP8X4),
                rhs_scale=x_plane[:, cols],
                start=(i == 0),
                stop=(i == 2),
            )

        for t in range(TILES):
            for c in range(2):
                second_pass(t, c, 0, w_k4, w_two[:], planes_x2[:, 0:S])

        last = TILES - 1
        z = work.tile([P, S, TILES], BF16, name="z", align_bytes=64)
        ub = {}
        far = {}
        far_tags = {(0, 0): "h1", (0, 1): "pb3", (1, 0): "excess_1_3", (1, 1): "pa3"}

        def finish_z(t):
            for c in range(2):
                cols = slice(c * HALF, (c + 1) * HALF)
                larger = work.tile([P, HALF], F32, align_bytes=64, name="larger", bufs=4)
                nc.vector.tensor_tensor(larger[:], ub[t][:, cols], far[t, c][:], ALU.max)
                nc.scalar.activation(z[:, cols, t], larger[:], COPY, scale=gain[:, t : t + 1])

        for t in range(TILES):
            ub[t] = work.tile([P, S], F32, name="ub", tag=("pb1", "ub1", "h1", "excess_1_3")[t], align_bytes=64)
            nc.vector.tensor_copy(ub[t][:].indirect(lists["n3"][:]), ra[t][:])
            nc.vector.tensor_copy(ub[t][:].indirect(lists["n4"][:]), rb[t][:])
            for c in range(2):
                far[t, c] = work.tile([P, HALF], F32, name="far", tag=far_tags.get((t, c), "far%d_%d" % (t, c)), align_bytes=64)
                nc.scalar.activation(far[t, c][:], ub[t][:].indirect(half_of("n5", c)), COPY)
            if t > 0:
                finish_z(t - 1)
        finish_z(last)
        w_k5 = gather_words(d_tab, "k5", tag="far%d_1" % (last - 1))
        w_hy = gather_words(x_tab, "hy", tag="rb%d" % last)
        w_k5 = deal_words(w_k5, "k5")
        for t in range(TILES):
            for c in range(2):
                second_pass(t, c, 1, w_k5, w_hy[:], planes_x2[:, S : 2 * S])
        w_k3 = deal_words(gather_words(d_tab, "k3", tag="far%d_1" % last), "k3")

        z_words = work.tile([P, S], U32, name="z_words", align_bytes=64)
        z_plane = work.tile([P, S], U8, name="z_plane", align_bytes=64)
        for c in range(2):
            cols = slice(c * HALF, (c + 1) * HALF)
            nc.vector.quantize_mx(
                out=z_words[:, cols].bitcast(FP8X4), scales=z_plane[:, cols], in_=z[:, cols, :].rearrange("p n t -> p (n t)")
            )

        pa2, pb2, ra2, rb2, excess_2 = [], [], [], [], {}
        for t in range(TILES):
            h2 = work.tile([P, S], F32, align_bytes=64, name="h2_%d" % t)
            pa2.append(work.tile([P, W], F32, align_bytes=64, name="pa2_%d" % t))
            pb2.append(work.tile([P, W], F32, align_bytes=64, name="pb2_%d" % t))
            for c in range(2):
                second_pass(t, c, 2, w_k3, z_words[:], z_plane[:])
            nc.scalar.activation(h2[:, 0:HALF], sums_2[t, 0][:], COPY, scale=SIXTEENTH)
            if t == 0:
                nc.vector.tensor_scalar_mul(h2[:, HALF:S], sums_2[t, 1][:], SIXTEENTH)
                nc.vector.tensor_copy(pa2[t][:], h2[:].indirect(lists["n6"][:]))
            else:
                nc.scalar.activation(h2[:, HALF:S], sums_2[t, 1][:], COPY, scale=SIXTEENTH)
                nc.scalar.activation(pa2[t][:], h2[:].indirect(lists["n6"][:]), COPY)
            nc.scalar.activation(pb2[t][:], h2[:].indirect(lists["n7"][:]), COPY)
            rb2.append(work.tile([P, W], F32, align_bytes=64, name="rb2_%d" % t))
            if t < 2:
                nc.vector.tensor_tensor(rb2[t][:], pa2[t][:], pb2[t][:], ALU.min)
            else:
                lead = work.tile([P, W], F32, align_bytes=64, name="lead%d" % t)
                nc.gpsimd.tensor_tensor(lead[:], pb2[t][:], pa2[t][:], ALU.subtract)
                excess_2[t] = excess_over("excess_2_%d" % t, lead[:])
                nc.gpsimd.tensor_tensor(rb2[t][:], pb2[t][:], excess_2[t][:], ALU.subtract)
        for t in range(TILES):
            ra2.append(work.tile([P, W], F32, align_bytes=64, name="ra2", tag=("h2_1", "ra2_1", "lead3", "ra2_3")[t]))
            if t < 2:
                nc.vector.tensor_tensor(ra2[t][:], pa2[t][:], pb2[t][:], ALU.max)
            else:
                nc.gpsimd.tensor_tensor(ra2[t][:], pa2[t][:], excess_2[t][:], ALU.add)

        out_rows = out.rearrange("(b t q) j -> t b q j", t=TILES, q=CHUNK)
        ub2 = [work.tile([P, S], F32, align_bytes=64, name="ub2_%d" % t) for t in range(TILES)]
        for pair in ((0, 1), (2, 3)):
            for t in pair:
                nc.vector.tensor_copy(ub2[t][:].indirect(lists["n7"][:]), rb2[t][:])
            for t in pair:
                nc.vector.tensor_copy(ub2[t][:].indirect(lists["n6"][:]), ra2[t][:])
        for t in range(TILES):
            other = work.tile([P, S], F32, align_bytes=64, name="other", tag=("pb2_3", "excess_2_2", "other2", "other3")[t])
            result = work.tile([P, S], F32, align_bytes=64, name="result", tag=("excess_2_3", "pa2_3", "ra2_3", "result3")[t])
            cuts = (0, HALF, S - P, S) if t == last else (0, HALF, S)
            for lo, hi in zip(cuts, cuts[1:]):
                cols = slice(lo, hi)
                nc.scalar.activation(other[:, cols], ub2[t][:].indirect(lists["n8"][:, lo // 16 : hi // 16]), COPY)
                if t == last:
                    nc.vector.tensor_tensor(result[:, cols], ub2[t][:, cols], other[:, cols], ALU.subtract)
                    nc.sync.dma_start(out_rows[t][:, :, cols], result[:, cols])
            if t < last:
                engine = nc.gpsimd if t < 2 else nc.vector
                engine.tensor_tensor(result[:], ub2[t][:], other[:], ALU.subtract)
                nc.sync.dma_start(out_rows[t], result[:])
